import numpy as np
import ml_dtypes


def mxq(x, axis, fmt="e4m3"):
    dtype, down = {"e4m3": (ml_dtypes.float8_e4m3fn, 7), "e5m2": (ml_dtypes.float8_e5m2, 14)}[fmt]
    v = np.moveaxis(np.asarray(x, np.float32).astype(ml_dtypes.bfloat16).astype(np.float64), axis, -1)
    blocks = v.reshape(v.shape[:-1] + (-1, 32))
    amax = np.abs(blocks).max(-1, keepdims=True)
    byte = np.maximum(np.where(amax > 0, np.frexp(amax)[1] - 1 + 127, 0) - down, 1)
    scale = np.exp2(byte - 127.0)
    codes = (blocks / scale).astype(np.float32).astype(dtype).astype(np.float64)
    return np.moveaxis((codes * scale).reshape(v.shape), -1, axis)


WIDE = False


def mx_kscale(k):
    if not WIDE:
        return np.ones(k)
    levels = np.array([10, -10, 5, -5, 0])
    if k % 512:
        return np.exp2(np.random.permutation(np.resize(levels, k // 32))).repeat(32)
    a = np.empty((k // 512, 16))
    for p in range(k // 512):
        a[p, :8] = np.random.permutation(np.resize(levels, 8))
        for g in range(8):
            far = levels[np.abs(levels - a[p, g]) >= 10]
            a[p, g + 8] = far[np.random.randint(len(far))]
    return np.exp2(a.ravel()).repeat(32)


def f64(x):
    return np.asarray(x).astype(np.float64)


def striped8(idx):
    return np.asarray(idx).reshape(8, -1, 16).transpose(0, 2, 1).reshape(128, -1).astype(np.uint16)


def unstriped8(offs):
    return offs.reshape(8, 16, -1).transpose(0, 2, 1).reshape(8, -1).astype(np.int64)


def pick8(x, idx, run):
    r = np.arange(len(x))
    return x[r[:, None], idx[r % (8 * run) // run]]


E2M1 = np.array([0.0, 0.5, 1.0, 1.5, 2.0, 3.0, 4.0, 6.0, -0.0, -0.5, -1.0, -1.5, -2.0, -3.0, -4.0, -6.0])


def pack_weight(w, fmt):
    k, n = w.shape
    w = f64(np.asarray(w, np.float32).astype(ml_dtypes.bfloat16)).reshape(k // 32, 32, n)
    amax = np.abs(w).max(1)
    if fmt == "e4m3":
        byte = np.frexp(amax)[1] - 1 + 127 - 7
    else:
        mant, ex = np.frexp(amax / 6.0)
        byte = np.where(mant > 0.5, ex, ex - 1) + 127
    byte = np.clip(np.where(amax > 0, byte, 1), 1, 254)
    scaled = (w * np.exp2(127.0 - byte)[:, None, :]).reshape(k, n).astype(np.float32)
    by_word = np.ascontiguousarray(scaled.reshape(k // 512, 128, 4, n).transpose(0, 1, 3, 2))
    if fmt == "e4m3":
        words = by_word.astype(ml_dtypes.float8_e4m3fn).view(np.uint8)
    else:
        c = by_word.astype(ml_dtypes.float4_e2m1fn).view(np.uint8) & 0xF
        words = (c[..., 0::2] | (c[..., 1::2] << 4)).reshape(k // 512, 128, 2 * n)
    return np.ascontiguousarray(words), np.ascontiguousarray(byte.astype(np.uint8).reshape(k // 512, 16, n))


def unpack_weight(words, scales, fmt):
    g, _, n = scales.shape
    words = np.ascontiguousarray(words).reshape(g, 128, n, -1)
    if fmt == "e4m3":
        vals = words.view(ml_dtypes.float8_e4m3fn).astype(np.float64)
    else:
        nib = np.empty((g, 128, n, 4), np.uint8)
        nib[..., 0::2] = words & 0xF
        nib[..., 1::2] = words >> 4
        vals = E2M1[nib]
    vals = vals * np.repeat(np.exp2(scales.astype(np.float64) - 127.0), 8, axis=1)[..., None]
    return vals.transpose(0, 1, 3, 2).reshape(g * 512, n)


D, T, I, Q, G = 512, 1024, 512, 128, 64


def setup_inputs():
    n = np.random.standard_normal
    idx = np.stack([np.random.permutation(T)[:I] for _ in range(8)])
    idx2 = np.stack([np.random.permutation(T)[:I] for _ in range(8)])
    fd = mx_kscale(D)
    keysp = pack_weight(n((D, T)) / fd[:, None], "e2m1")
    return {
        "query": (n((D, Q)) * 0.9 / np.sqrt(D) * fd[:, None]).astype(np.float32),
        "query2": (n((D, Q)) * 0.9 / np.sqrt(D) * fd[:, None]).astype(np.float32),
        "keys_words": keysp[0],
        "keys_scales": keysp[1],
        "base": (0.3 * n((Q, I))).astype(np.float32),
        "gain2": (np.random.uniform(0.5, 2.0, (Q, 1))).astype(np.float32),
        "offs": striped8(idx),
        "offs2": striped8(idx2),
    }


def reference(query, query2, keys_words, keys_scales, base, gain2, offs, offs2):
    idx = unstriped8(offs)
    idx2 = unstriped8(offs2)
    keysu = unpack_weight(keys_words, keys_scales, "e2m1")
    queryq = mxq(f64(query), 0, "e4m3")
    a = queryq.T @ keysu
    query2q = mxq(f64(query2), 0, "e4m3")
    b = query2q.T @ keysu
    s = pick8(a, idx, 16) * pick8(b, idx2, 16) - pick8(b, idx, 16) * pick8(a, idx2, 16)
    p = np.exp(s)
    pg = p.reshape(Q, G, I // G).sum(axis=2)
    k0 = np.tanh(pg / np.mean(pg, axis=1, keepdims=True)) / pg / 64.0
    kr = np.repeat(k0, I // G, axis=1)
    w = p * kr
    y = np.tanh(w * f64(gain2) * 256.0) + f64(base)
    return y

@@ -1,0 +1,216 @@
+from contextlib import ExitStack
+
+import concourse.mybir as mybir
+
+F32 = mybir.dt.float32
+BF16 = mybir.dt.bfloat16
+I32 = mybir.dt.int32
+U32 = mybir.dt.uint32
+U16 = mybir.dt.uint16
+U8 = mybir.dt.uint8
+FP8X4 = mybir.dt.float8_e4m3fn_x4
+FP4X4 = mybir.dt.float4_e2m1fn_x4
+ALU = mybir.AluOpType
+ACT = mybir.ActivationFunctionType
+AXIS_X = mybir.AxisListType.X
+
+P = 128
+D, T, SLOTS, Q, RUNS = 512, 1024, 512, 128, 64
+RUN = SLOTS // RUNS
+PACK = 4
+PASS_EDGES = (0, 256, 512, 768, 896, 1024)
+HALF = SLOTS // 2
+HALF_RUNS = RUNS // 2
+LIST_COLS = HALF // 16
+RECIP_CAP = 1.0e30
+
+FLOPS = 2 * 2 * D * Q * T
+
+
+def tile_attend_wedge_evenruns_gated_heads_kernel(
+    tc, query, query2, keys_words, keys_scales, base, gain2, offs, offs2, out
+):
+    nc = tc.nc
+    with ExitStack() as ctx:
+        sb = ctx.enter_context(tc.tile_pool(name="sb", bufs=1))
+        psum = ctx.enter_context(tc.psum_pool(name="psum", bufs=1))
+
+        list1 = sb.tile([P, SLOTS // 16], U16, name="list1")
+        list2 = sb.tile([P, SLOTS // 16], U16, name="list2")
+        raw = [sb.tile([P, PACK, Q], F32, name="raw%d" % u) for u in range(2)]
+        k_words = sb.tile([P, 2 * T], U8, name="k_words", align_bytes=64)
+        k_scales = sb.tile([P, T], U8, name="k_scales", align_bytes=64)
+        base_t = sb.tile([P, SLOTS], F32, name="base_t")
+        gain_t = sb.tile([P, 1], F32, name="gain_t")
+
+        nc.vector.memset(k_scales[:].bitcast(I32), 0)
+        nc.sync.dma_start(out=raw[0][:], in_=query.rearrange("(p j) q -> p j q", j=PACK))
+        scale_rows = keys_scales[0].bitcast(I32).rearrange("(g r) c -> r g c", r=4)
+        for r in range(4):
+            nc.sync.dma_start(out=k_scales[r:P:32, :].bitcast(I32), in_=scale_rows[r])
+        words = keys_words[0].bitcast(I32)
+        k_words_i = k_words[:].bitcast(I32)
+        nc.sync.dma_start(out=k_words_i[:, 0 : T // 4], in_=words[:, 0 : T // 4])
+        nc.sync.dma_start(out=raw[1][:], in_=query2.rearrange("(p j) q -> p j q", j=PACK))
+        nc.sync.dma_start(out=k_words_i[:, T // 4 : T // 2], in_=words[:, T // 4 : T // 2])
+        nc.sync.dma_start(list1[:], offs)
+        nc.sync.dma_start(list2[:], offs2)
+        nc.sync.dma_start(out=base_t[:], in_=base)
+        nc.sync.dma_start(out=gain_t[:], in_=gain2)
+
+        scores = []
+        for u in range(2):
+            grouped = sb.tile([P, Q, PACK], BF16, name="grouped%d" % u, align_bytes=64)
+            nc.vector.tensor_copy(
+                out=grouped[:].rearrange("p (c i) j -> p c j i", i=4),
+                in_=raw[u][:].rearrange("p j (c i) -> p c j i", i=4),
+            )
+            codes = sb.tile([P, Q], U32, name="codes%d" % u, align_bytes=64)
+            q_scales = sb.tile([P, Q], U8, name="q_scales%d" % u, align_bytes=64)
+            nc.vector.quantize_mx(
+                out=codes[:].bitcast(FP8X4),
+                scales=q_scales[:],
+                in_=grouped[:].rearrange("p q j -> p (q j)"),
+            )
+            table = sb.tile([P, T], F32, name="scores%d" % u)
+            for c, (t0, t1) in enumerate(zip(PASS_EDGES[:-1], PASS_EDGES[1:])):
+                cols = slice(t0, t1)
+                bank = psum.tile([P, t1 - t0], F32, name="bank%d" % ((u * (len(PASS_EDGES) - 1) + c) % 8))
+                nc.tensor.matmul_mx(
+                    out=bank[:],
+                    lhsT=codes[:].bitcast(FP8X4),
+                    lhsT_scale=q_scales[:],
+                    rhs=k_words[:, 2 * cols.start : 2 * cols.stop].bitcast(FP4X4),
+                    rhs_scale=k_scales[:, cols],
+                    start=True,
+                    stop=True,
+                )
+                if u == 0:
+                    nc.scalar.activation(out=table[:, cols], in_=bank[:], func=ACT.Copy)
+                else:
+                    nc.vector.tensor_copy(out=table[:, cols], in_=bank[:])
+            scores.append(table)
+        a, b = scores
+
+        def half_tile(name):
+            return sb.tile([P, HALF], F32, name=name)
+
+        def column(name):
+            return sb.tile([P, 1], F32, name=name)
+
+        def looked_up(table, lists, h):
+            return table[:].indirect(lists[:, h * LIST_COLS : (h + 1) * LIST_COLS])
+
+        def gather(name, table, lists, h):
+            picked = half_tile(name)
+            nc.scalar.activation(out=picked[:], in_=looked_up(table, lists, h), func=ACT.Copy)
+            return picked
+
+        def gather_times(name, table, lists, h, other):
+            product = half_tile(name)
+            nc.vector.tensor_tensor(product[:], looked_up(table, lists, h), other[:], ALU.mult)
+            return product
+
+        def binary(name, x, y, op):
+            result = half_tile(name)
+            nc.vector.tensor_tensor(result[:], x[:], y[:], op)
+            return result
+
+        def negate_with_min(name, s, start):
+            neg = half_tile(name)
+            least = column(name + "_min")
+            nc.vector.tensor_scalar(
+                out=neg[:], in0=s[:], scalar1=-1.0, scalar2=start, op0=ALU.mult, op1=ALU.min, accum_out=least[:]
+            )
+            return neg, least
+
+        a1_0 = gather("a1_0", a, list1, 0)
+        a2_0 = gather("a2_0", a, list2, 0)
+        a2_1 = gather("a2_1", a, list2, 1)
+        a1_1 = gather("a1_1", a, list1, 1)
+        b2_1 = gather("b2_1", b, list2, 1)
+        left_0 = gather_times("left_0", b, list2, 0, a1_0)
+        right_0 = gather_times("right_0", b, list1, 0, a2_0)
+        right_1 = gather_times("right_1", b, list1, 1, a2_1)
+        s_0 = binary("s_0", left_0, right_0, ALU.subtract)
+        left_1 = binary("left_1", a1_1, b2_1, ALU.mult)
+        neg_s0, neg_max0 = negate_with_min("neg_s0", s_0, None)
+        s_1 = binary("s_1", left_1, right_1, ALU.subtract)
+        neg_s1, neg_max = negate_with_min("neg_s1", s_1, neg_max0[:])
+
+        p = sb.tile([P, RUNS, RUN], F32, name="p")
+        first, second = slice(0, HALF_RUNS), slice(HALF_RUNS, RUNS)
+        nc.scalar.activation(
+            out=p[:, first, :].rearrange("p g e -> p (g e)"), in_=neg_s0[:], func=ACT.Exp, bias=neg_max0[:], scale=-1.0
+        )
+        rescale = column("rescale")
+        nc.scalar.activation(out=rescale[:], in_=neg_max0[:], func=ACT.Exp, bias=neg_max[:], scale=-1.0)
+        sum_1 = column("sum_1")
+        nc.scalar.activation(
+            out=p[:, second, :].rearrange("p g e -> p (g e)"),
+            in_=neg_s1[:],
+            func=ACT.Exp,
+            bias=neg_max[:],
+            scale=-1.0,
+            accum_out=sum_1[:],
+        )
+
+        pg_0 = s_1[:, 0:HALF_RUNS]
+        pg = sb.tile([P, RUNS], F32, name="pg")
+        inv_pg = sb.tile([P, RUNS], F32, name="inv_pg")
+        nc.vector.tensor_reduce(out=pg_0, in_=p[:, first, :], axis=AXIS_X, op=ALU.add)
+        sum_0 = column("sum_0")
+        nc.vector.tensor_scalar(
+            out=pg[:, first], in0=pg_0, scalar1=rescale[:], scalar2=None, op0=ALU.mult, op1=ALU.add, accum_out=sum_0[:]
+        )
+        nc.vector.reciprocal(out=inv_pg[:, first], in_=pg_0)
+        nc.vector.tensor_reduce(out=pg[:, second], in_=p[:, second, :], axis=AXIS_X, op=ALU.add)
+        mean = column("mean")
+        nc.vector.tensor_scalar(
+            out=mean[:], in0=sum_1[:], scalar1=sum_0[:], scalar2=1.0 / RUNS, op0=ALU.add, op1=ALU.mult
+        )
+        inv_mean = column("inv_mean")
+        nc.vector.reciprocal(out=inv_mean[:], in_=mean[:])
+        nc.vector.reciprocal(out=inv_pg[:, second], in_=pg[:, second])
+        share_0 = sb.tile([P, HALF_RUNS, RUN], F32, name="share_0")
+        nc.vector.scalar_tensor_tensor(
+            out=share_0[:],
+            in0=inv_pg[:, first].unsqueeze(2).to_broadcast([P, HALF_RUNS, RUN]),
+            scalar=RECIP_CAP,
+            in1=p[:, first, :],
+            op0=ALU.min,
+            op1=ALU.mult,
+        )
+        gate = sb.tile([P, RUNS], F32, name="gate")
+        nc.scalar.activation(out=gate[:], in_=pg[:], func=ACT.Tanh, scale=inv_mean[:])
+        k_1 = sb.tile([P, HALF_RUNS], F32, name="k_1")
+        nc.vector.scalar_tensor_tensor(
+            out=k_1[:], in0=inv_pg[:, second], scalar=RECIP_CAP, in1=gate[:, second], op0=ALU.min, op1=ALU.mult
+        )
+
+        edges = [0,16,32,48,64]
+        spans = list(zip(edges[:-1], edges[1:]))
+        th = []
+        for n, (g0, g1) in enumerate(spans):
+            if g0 < HALF_RUNS:
+                values, factor = share_0[:, g0:g1, :], gate[:, g0:g1]
+            else:
+                values, factor = p[:, g0:g1, :], k_1[:, g0 - HALF_RUNS : g1 - HALF_RUNS]
+            w = sb.tile([P, g1 - g0, RUN], F32, name="w_%d" % n)
+            nc.vector.scalar_tensor_tensor(
+                out=w[:],
+                in0=values,
+                scalar=256.0 / RUNS,
+                in1=factor.unsqueeze(2).to_broadcast([P, g1 - g0, RUN]),
+                op0=ALU.mult,
+                op1=ALU.mult,
+            )
+            th.append(sb.tile([P, (g1 - g0) * RUN], F32, name="th_%d" % n))
+            nc.scalar.activation(
+                out=th[n][:], in_=w[:].rearrange("p g e -> p (g e)"), func=ACT.Tanh, scale=gain_t[:]
+            )
+        for n, (g0, g1) in enumerate(spans):
+            cols = slice(g0 * RUN, g1 * RUN)
+            y = sb.tile([P, (g1 - g0) * RUN], F32, name="y_%d" % n)
+            nc.vector.tensor_tensor(y[:], th[n][:], base_t[:, cols], ALU.add)
+            nc.sync.dma_start(out=out[:, cols], in_=y[:])

@@ -23,6 +23,7 @@ HALF = SLOTS // 2
 HALF_RUNS = RUNS // 2
 LIST_COLS = HALF // 16
 RECIP_CAP = 1.0e30
+GAP_CAP = 64.0
 
 FLOPS = 2 * 2 * D * Q * T
 
@@ -45,12 +46,13 @@ def tile_attend_wedge_evenruns_gated_heads_kernel(
 
         nc.vector.memset(k_scales[:].bitcast(I32), 0)
         nc.sync.dma_start(out=raw[0][:], in_=query.rearrange("(p j) q -> p j q", j=PACK))
-        scale_rows = keys_scales[0].bitcast(I32).rearrange("(g r) c -> r g c", r=4)
-        for r in range(4):
-            nc.sync.dma_start(out=k_scales[r:P:32, :].bitcast(I32), in_=scale_rows[r])
         words = keys_words[0].bitcast(I32)
         k_words_i = k_words[:].bitcast(I32)
         nc.sync.dma_start(out=k_words_i[:, 0 : T // 4], in_=words[:, 0 : T // 4])
+        scale_rows = keys_scales[0].bitcast(I32).rearrange("(g r) c -> r g c", r=4)
+        for r in range(4):
+            queue = nc.sync if r % 2 == 0 else nc.scalar
+            queue.dma_start(out=k_scales[r:P:32, :].bitcast(I32), in_=scale_rows[r])
         nc.sync.dma_start(out=raw[1][:], in_=query2.rearrange("(p j) q -> p j q", j=PACK))
         nc.sync.dma_start(out=k_words_i[:, T // 4 : T // 2], in_=words[:, T // 4 : T // 2])
         nc.sync.dma_start(list1[:], offs)
@@ -61,17 +63,19 @@ def tile_attend_wedge_evenruns_gated_heads_kernel(
         scores = []
         for u in range(2):
             grouped = sb.tile([P, Q, PACK], BF16, name="grouped%d" % u, align_bytes=64)
-            nc.vector.tensor_copy(
-                out=grouped[:].rearrange("p (c i) j -> p c j i", i=4),
-                in_=raw[u][:].rearrange("p j (c i) -> p c j i", i=4),
-            )
+            for q0 in (0, Q // 2):
+                nc.vector.tensor_copy(
+                    out=grouped[:, q0 : q0 + Q // 2, :].rearrange("p (c i) j -> p c j i", i=4),
+                    in_=raw[u][:, :, q0 : q0 + Q // 2].rearrange("p j (c i) -> p c j i", i=4),
+                )
             codes = sb.tile([P, Q], U32, name="codes%d" % u, align_bytes=64)
             q_scales = sb.tile([P, Q], U8, name="q_scales%d" % u, align_bytes=64)
-            nc.vector.quantize_mx(
-                out=codes[:].bitcast(FP8X4),
-                scales=q_scales[:],
-                in_=grouped[:].rearrange("p q j -> p (q j)"),
-            )
+            for q0 in (0, Q // 2):
+                nc.vector.quantize_mx(
+                    out=codes[:, q0 : q0 + Q // 2].bitcast(FP8X4),
+                    scales=q_scales[:, q0 : q0 + Q // 2],
+                    in_=grouped[:, q0 : q0 + Q // 2, :].rearrange("p q j -> p (q j)"),
+                )
             table = sb.tile([P, T], F32, name="scores%d" % u)
             for c, (t0, t1) in enumerate(zip(PASS_EDGES[:-1], PASS_EDGES[1:])):
                 cols = slice(t0, t1)
@@ -85,10 +89,7 @@ def tile_attend_wedge_evenruns_gated_heads_kernel(
                     start=True,
                     stop=True,
                 )
-                if u == 0:
-                    nc.scalar.activation(out=table[:, cols], in_=bank[:], func=ACT.Copy)
-                else:
-                    nc.vector.tensor_copy(out=table[:, cols], in_=bank[:])
+                nc.scalar.activation(out=table[:, cols], in_=bank[:], func=ACT.Copy)
             scores.append(table)
         a, b = scores
 
@@ -106,6 +107,11 @@ def tile_attend_wedge_evenruns_gated_heads_kernel(
             nc.scalar.activation(out=picked[:], in_=looked_up(table, lists, h), func=ACT.Copy)
             return picked
 
+        def gather_on_vector(name, table, lists, h):
+            picked = half_tile(name)
+            nc.vector.tensor_copy(picked[:], looked_up(table, lists, h))
+            return picked
+
         def gather_times(name, table, lists, h, other):
             product = half_tile(name)
             nc.vector.tensor_tensor(product[:], looked_up(table, lists, h), other[:], ALU.mult)
@@ -116,62 +122,66 @@ def tile_attend_wedge_evenruns_gated_heads_kernel(
             nc.vector.tensor_tensor(result[:], x[:], y[:], op)
             return result
 
-        def negate_with_min(name, s, start):
-            neg = half_tile(name)
-            least = column(name + "_min")
-            nc.vector.tensor_scalar(
-                out=neg[:], in0=s[:], scalar1=-1.0, scalar2=start, op0=ALU.mult, op1=ALU.min, accum_out=least[:]
-            )
-            return neg, least
-
-        a1_0 = gather("a1_0", a, list1, 0)
-        a2_0 = gather("a2_0", a, list2, 0)
+        a1_0 = gather_on_vector("a1_0", a, list1, 0)
+        a2_0 = gather_on_vector("a2_0", a, list2, 0)
         a2_1 = gather("a2_1", a, list2, 1)
         a1_1 = gather("a1_1", a, list1, 1)
         b2_1 = gather("b2_1", b, list2, 1)
         left_0 = gather_times("left_0", b, list2, 0, a1_0)
         right_0 = gather_times("right_0", b, list1, 0, a2_0)
         right_1 = gather_times("right_1", b, list1, 1, a2_1)
-        s_0 = binary("s_0", left_0, right_0, ALU.subtract)
         left_1 = binary("left_1", a1_1, b2_1, ALU.mult)
-        neg_s0, neg_max0 = negate_with_min("neg_s0", s_0, None)
-        s_1 = binary("s_1", left_1, right_1, ALU.subtract)
-        neg_s1, neg_max = negate_with_min("neg_s1", s_1, neg_max0[:])
+        neg_s = [binary("neg_s0", right_0, left_0, ALU.subtract), binary("neg_s1", right_1, left_1, ALU.subtract)]
+        halves = (slice(0, HALF_RUNS), slice(HALF_RUNS, RUNS))
+        first, second = halves
+        neg_max = sb.tile([P, 2], F32, name="neg_max")
+        for h in range(2):
+            nc.vector.tensor_reduce(out=neg_max[:, h : h + 1], in_=neg_s[h][:], axis=AXIS_X, op=ALU.min)
+        gap = column("gap")
+        nc.vector.tensor_scalar(
+            out=gap[:], in0=neg_max[:, 1:2], scalar1=neg_max[:, 0:1], scalar2=GAP_CAP, op0=ALU.subtract, op1=ALU.min
+        )
 
         p = sb.tile([P, RUNS, RUN], F32, name="p")
-        first, second = slice(0, HALF_RUNS), slice(HALF_RUNS, RUNS)
-        nc.scalar.activation(
-            out=p[:, first, :].rearrange("p g e -> p (g e)"), in_=neg_s0[:], func=ACT.Exp, bias=neg_max0[:], scale=-1.0
-        )
+        half_sum = sb.tile([P, 2], F32, name="half_sum")
+        for h in range(2):
+            nc.scalar.activation(
+                out=p[:, halves[h], :].rearrange("p g e -> p (g e)"),
+                in_=neg_s[h][:],
+                func=ACT.Exp,
+                bias=neg_max[:, h : h + 1],
+                scale=-1.0,
+                accum_out=half_sum[:, h : h + 1],
+            )
         rescale = column("rescale")
-        nc.scalar.activation(out=rescale[:], in_=neg_max0[:], func=ACT.Exp, bias=neg_max[:], scale=-1.0)
-        sum_1 = column("sum_1")
-        nc.scalar.activation(
-            out=p[:, second, :].rearrange("p g e -> p (g e)"),
-            in_=neg_s1[:],
-            func=ACT.Exp,
-            bias=neg_max[:],
-            scale=-1.0,
-            accum_out=sum_1[:],
-        )
+        nc.scalar.activation(out=rescale[:], in_=gap[:], func=ACT.Exp)
+        rescale_runs = column("rescale_runs")
+        nc.scalar.activation(out=rescale_runs[:], in_=rescale[:], func=ACT.Copy, scale=float(RUNS))
 
-        pg_0 = s_1[:, 0:HALF_RUNS]
         pg = sb.tile([P, RUNS], F32, name="pg")
+        pg_row = sb.tile([P, RUNS], F32, name="pg_row")
         inv_pg = sb.tile([P, RUNS], F32, name="inv_pg")
-        nc.vector.tensor_reduce(out=pg_0, in_=p[:, first, :], axis=AXIS_X, op=ALU.add)
-        sum_0 = column("sum_0")
+        for h in range(2):
+            nc.vector.tensor_reduce(out=pg[:, halves[h]], in_=p[:, halves[h], :], axis=AXIS_X, op=ALU.add)
+            nc.scalar.activation(
+                out=pg_row[:, halves[h]],
+                in_=pg[:, halves[h]],
+                func=ACT.Copy,
+                scale=rescale_runs[:] if h == 0 else float(RUNS),
+            )
+        mean = column("row_sum")
         nc.vector.tensor_scalar(
-            out=pg[:, first], in0=pg_0, scalar1=rescale[:], scalar2=None, op0=ALU.mult, op1=ALU.add, accum_out=sum_0[:]
-        )
-        nc.vector.reciprocal(out=inv_pg[:, first], in_=pg_0)
-        nc.vector.tensor_reduce(out=pg[:, second], in_=p[:, second, :], axis=AXIS_X, op=ALU.add)
-        mean = column("mean")
-        nc.vector.tensor_scalar(
-            out=mean[:], in0=sum_1[:], scalar1=sum_0[:], scalar2=1.0 / RUNS, op0=ALU.add, op1=ALU.mult
+            out=mean[:],
+            in0=half_sum[:, 0:1],
+            scalar1=rescale[:],
+            scalar2=half_sum[:, 1:2],
+            op0=ALU.mult,
+            op1=ALU.add,
         )
         inv_mean = column("inv_mean")
         nc.vector.reciprocal(out=inv_mean[:], in_=mean[:])
-        nc.vector.reciprocal(out=inv_pg[:, second], in_=pg[:, second])
+        for h in range(2):
+            nc.vector.reciprocal(out=inv_pg[:, halves[h]], in_=pg[:, halves[h]])
         share_0 = sb.tile([P, HALF_RUNS, RUN], F32, name="share_0")
         nc.vector.scalar_tensor_tensor(
             out=share_0[:],
@@ -182,7 +192,7 @@ def tile_attend_wedge_evenruns_gated_heads_kernel(
             op1=ALU.mult,
         )
         gate = sb.tile([P, RUNS], F32, name="gate")
-        nc.scalar.activation(out=gate[:], in_=pg[:], func=ACT.Tanh, scale=inv_mean[:])
+        nc.scalar.activation(out=gate[:], in_=pg_row[:], func=ACT.Tanh, scale=inv_mean[:])
         k_1 = sb.tile([P, HALF_RUNS], F32, name="k_1")
         nc.vector.scalar_tensor_tensor(
             out=k_1[:], in0=inv_pg[:, second], scalar=RECIP_CAP, in1=gate[:, second], op0=ALU.min, op1=ALU.mult

from contextlib import ExitStack

import concourse.mybir as mybir

F32 = mybir.dt.float32
BF16 = mybir.dt.bfloat16
I32 = mybir.dt.int32
U32 = mybir.dt.uint32
U16 = mybir.dt.uint16
U8 = mybir.dt.uint8
FP8X4 = mybir.dt.float8_e4m3fn_x4
FP4X4 = mybir.dt.float4_e2m1fn_x4
ALU = mybir.AluOpType
ACT = mybir.ActivationFunctionType
AXIS_X = mybir.AxisListType.X

P = 128
D, T, SLOTS, Q, RUNS = 512, 1024, 512, 128, 64
RUN = SLOTS // RUNS
PACK = 4
PASS_EDGES = (0, 256, 512, 768, 896, 1024)
HALF = SLOTS // 2
HALF_RUNS = RUNS // 2
LIST_COLS = HALF // 16
RECIP_CAP = 1.0e30
GAP_CAP = 64.0

FLOPS = 2 * 2 * D * Q * T


def tile_attend_wedge_evenruns_gated_heads_kernel(
    tc, query, query2, keys_words, keys_scales, base, gain2, offs, offs2, out
):
    nc = tc.nc
    with ExitStack() as ctx:
        sb = ctx.enter_context(tc.tile_pool(name="sb", bufs=1))
        psum = ctx.enter_context(tc.psum_pool(name="psum", bufs=1))

        list1 = sb.tile([P, SLOTS // 16], U16, name="list1")
        list2 = sb.tile([P, SLOTS // 16], U16, name="list2")
        raw = [sb.tile([P, PACK, Q], F32, name="raw%d" % u) for u in range(2)]
        k_words = sb.tile([P, 2 * T], U8, name="k_words", align_bytes=64)
        k_scales = sb.tile([P, T], U8, name="k_scales", align_bytes=64)
        base_t = sb.tile([P, SLOTS], F32, name="base_t")
        gain_t = sb.tile([P, 1], F32, name="gain_t")

        nc.vector.memset(k_scales[:].bitcast(I32), 0)
        nc.sync.dma_start(out=raw[0][:], in_=query.rearrange("(p j) q -> p j q", j=PACK))
        words = keys_words[0].bitcast(I32)
        k_words_i = k_words[:].bitcast(I32)
        nc.sync.dma_start(out=k_words_i[:, 0 : T // 4], in_=words[:, 0 : T // 4])
        scale_rows = keys_scales[0].bitcast(I32).rearrange("(g r) c -> r g c", r=4)
        for r in range(4):
            queue = nc.sync if r % 2 == 0 else nc.scalar
            queue.dma_start(out=k_scales[r:P:32, :].bitcast(I32), in_=scale_rows[r])
        nc.sync.dma_start(out=raw[1][:], in_=query2.rearrange("(p j) q -> p j q", j=PACK))
        nc.sync.dma_start(out=k_words_i[:, T // 4 : T // 2], in_=words[:, T // 4 : T // 2])
        nc.sync.dma_start(list1[:], offs)
        nc.sync.dma_start(list2[:], offs2)
        nc.sync.dma_start(out=base_t[:], in_=base)
        nc.sync.dma_start(out=gain_t[:], in_=gain2)

        scores = []
        for u in range(2):
            grouped = sb.tile([P, Q, PACK], BF16, name="grouped%d" % u, align_bytes=64)
            for q0 in (0, Q // 2):
                nc.vector.tensor_copy(
                    out=grouped[:, q0 : q0 + Q // 2, :].rearrange("p (c i) j -> p c j i", i=4),
                    in_=raw[u][:, :, q0 : q0 + Q // 2].rearrange("p j (c i) -> p c j i", i=4),
                )
            codes = sb.tile([P, Q], U32, name="codes%d" % u, align_bytes=64)
            q_scales = sb.tile([P, Q], U8, name="q_scales%d" % u, align_bytes=64)
            for q0 in (0, Q // 2):
                nc.vector.quantize_mx(
                    out=codes[:, q0 : q0 + Q // 2].bitcast(FP8X4),
                    scales=q_scales[:, q0 : q0 + Q // 2],
                    in_=grouped[:, q0 : q0 + Q // 2, :].rearrange("p q j -> p (q j)"),
                )
            table = sb.tile([P, T], F32, name="scores%d" % u)
            for c, (t0, t1) in enumerate(zip(PASS_EDGES[:-1], PASS_EDGES[1:])):
                cols = slice(t0, t1)
                bank = psum.tile([P, t1 - t0], F32, name="bank%d" % ((u * (len(PASS_EDGES) - 1) + c) % 8))
                nc.tensor.matmul_mx(
                    out=bank[:],
                    lhsT=codes[:].bitcast(FP8X4),
                    lhsT_scale=q_scales[:],
                    rhs=k_words[:, 2 * cols.start : 2 * cols.stop].bitcast(FP4X4),
                    rhs_scale=k_scales[:, cols],
                    start=True,
                    stop=True,
                )
                nc.scalar.activation(out=table[:, cols], in_=bank[:], func=ACT.Copy)
            scores.append(table)
        a, b = scores

        def half_tile(name):
            return sb.tile([P, HALF], F32, name=name)

        def column(name):
            return sb.tile([P, 1], F32, name=name)

        def looked_up(table, lists, h):
            return table[:].indirect(lists[:, h * LIST_COLS : (h + 1) * LIST_COLS])

        def gather(name, table, lists, h):
            picked = half_tile(name)
            nc.scalar.activation(out=picked[:], in_=looked_up(table, lists, h), func=ACT.Copy)
            return picked

        def gather_on_vector(name, table, lists, h):
            picked = half_tile(name)
            nc.vector.tensor_copy(picked[:], looked_up(table, lists, h))
            return picked

        def gather_times(name, table, lists, h, other):
            product = half_tile(name)
            nc.vector.tensor_tensor(product[:], looked_up(table, lists, h), other[:], ALU.mult)
            return product

        def binary(name, x, y, op):
            result = half_tile(name)
            nc.vector.tensor_tensor(result[:], x[:], y[:], op)
            return result

        a1_0 = gather_on_vector("a1_0", a, list1, 0)
        a2_0 = gather_on_vector("a2_0", a, list2, 0)
        a2_1 = gather("a2_1", a, list2, 1)
        a1_1 = gather("a1_1", a, list1, 1)
        b2_1 = gather("b2_1", b, list2, 1)
        left_0 = gather_times("left_0", b, list2, 0, a1_0)
        right_0 = gather_times("right_0", b, list1, 0, a2_0)
        right_1 = gather_times("right_1", b, list1, 1, a2_1)
        left_1 = binary("left_1", a1_1, b2_1, ALU.mult)
        neg_s = [binary("neg_s0", right_0, left_0, ALU.subtract), binary("neg_s1", right_1, left_1, ALU.subtract)]
        halves = (slice(0, HALF_RUNS), slice(HALF_RUNS, RUNS))
        first, second = halves
        neg_max = sb.tile([P, 2], F32, name="neg_max")
        for h in range(2):
            nc.vector.tensor_reduce(out=neg_max[:, h : h + 1], in_=neg_s[h][:], axis=AXIS_X, op=ALU.min)
        gap = column("gap")
        nc.vector.tensor_scalar(
            out=gap[:], in0=neg_max[:, 1:2], scalar1=neg_max[:, 0:1], scalar2=GAP_CAP, op0=ALU.subtract, op1=ALU.min
        )

        p = sb.tile([P, RUNS, RUN], F32, name="p")
        half_sum = sb.tile([P, 2], F32, name="half_sum")
        for h in range(2):
            nc.scalar.activation(
                out=p[:, halves[h], :].rearrange("p g e -> p (g e)"),
                in_=neg_s[h][:],
                func=ACT.Exp,
                bias=neg_max[:, h : h + 1],
                scale=-1.0,
                accum_out=half_sum[:, h : h + 1],
            )
        rescale = column("rescale")
        nc.scalar.activation(out=rescale[:], in_=gap[:], func=ACT.Exp)
        rescale_runs = column("rescale_runs")
        nc.scalar.activation(out=rescale_runs[:], in_=rescale[:], func=ACT.Copy, scale=float(RUNS))

        pg = sb.tile([P, RUNS], F32, name="pg")
        pg_row = sb.tile([P, RUNS], F32, name="pg_row")
        inv_pg = sb.tile([P, RUNS], F32, name="inv_pg")
        for h in range(2):
            nc.vector.tensor_reduce(out=pg[:, halves[h]], in_=p[:, halves[h], :], axis=AXIS_X, op=ALU.add)
            nc.scalar.activation(
                out=pg_row[:, halves[h]],
                in_=pg[:, halves[h]],
                func=ACT.Copy,
                scale=rescale_runs[:] if h == 0 else float(RUNS),
            )
        mean = column("row_sum")
        nc.vector.tensor_scalar(
            out=mean[:],
            in0=half_sum[:, 0:1],
            scalar1=rescale[:],
            scalar2=half_sum[:, 1:2],
            op0=ALU.mult,
            op1=ALU.add,
        )
        inv_mean = column("inv_mean")
        nc.vector.reciprocal(out=inv_mean[:], in_=mean[:])
        for h in range(2):
            nc.vector.reciprocal(out=inv_pg[:, halves[h]], in_=pg[:, halves[h]])
        share_0 = sb.tile([P, HALF_RUNS, RUN], F32, name="share_0")
        nc.vector.scalar_tensor_tensor(
            out=share_0[:],
            in0=inv_pg[:, first].unsqueeze(2).to_broadcast([P, HALF_RUNS, RUN]),
            scalar=RECIP_CAP,
            in1=p[:, first, :],
            op0=ALU.min,
            op1=ALU.mult,
        )
        gate = sb.tile([P, RUNS], F32, name="gate")
        nc.scalar.activation(out=gate[:], in_=pg_row[:], func=ACT.Tanh, scale=inv_mean[:])
        k_1 = sb.tile([P, HALF_RUNS], F32, name="k_1")
        nc.vector.scalar_tensor_tensor(
            out=k_1[:], in0=inv_pg[:, second], scalar=RECIP_CAP, in1=gate[:, second], op0=ALU.min, op1=ALU.mult
        )

        edges = [0,16,32,48,64]
        spans = list(zip(edges[:-1], edges[1:]))
        th = []
        for n, (g0, g1) in enumerate(spans):
            if g0 < HALF_RUNS:
                values, factor = share_0[:, g0:g1, :], gate[:, g0:g1]
            else:
                values, factor = p[:, g0:g1, :], k_1[:, g0 - HALF_RUNS : g1 - HALF_RUNS]
            w = sb.tile([P, g1 - g0, RUN], F32, name="w_%d" % n)
            nc.vector.scalar_tensor_tensor(
                out=w[:],
                in0=values,
                scalar=256.0 / RUNS,
                in1=factor.unsqueeze(2).to_broadcast([P, g1 - g0, RUN]),
                op0=ALU.mult,
                op1=ALU.mult,
            )
            th.append(sb.tile([P, (g1 - g0) * RUN], F32, name="th_%d" % n))
            nc.scalar.activation(
                out=th[n][:], in_=w[:].rearrange("p g e -> p (g e)"), func=ACT.Tanh, scale=gain_t[:]
            )
        for n, (g0, g1) in enumerate(spans):
            cols = slice(g0 * RUN, g1 * RUN)
            y = sb.tile([P, (g1 - g0) * RUN], F32, name="y_%d" % n)
            nc.vector.tensor_tensor(y[:], th[n][:], base_t[:, cols], ALU.add)
            nc.sync.dma_start(out=out[:, cols], in_=y[:])
